import numpy as np
import ml_dtypes


def mxq(x, axis, fmt="e4m3"):
    dtype, down = {"e4m3": (ml_dtypes.float8_e4m3fn, 7), "e5m2": (ml_dtypes.float8_e5m2, 14)}[fmt]
    v = np.moveaxis(np.asarray(x, np.float32).astype(ml_dtypes.bfloat16).astype(np.float64), axis, -1)
    blocks = v.reshape(v.shape[:-1] + (-1, 32))
    amax = np.abs(blocks).max(-1, keepdims=True)
    byte = np.maximum(np.where(amax > 0, np.frexp(amax)[1] - 1 + 127, 0) - down, 1)
    scale = np.exp2(byte - 127.0)
    codes = (blocks / scale).astype(np.float32).astype(dtype).astype(np.float64)
    return np.moveaxis((codes * scale).reshape(v.shape), -1, axis)


WIDE = False


def mx_kscale(k):
    if not WIDE:
        return np.ones(k)
    levels = np.array([10, -10, 5, -5, 0])
    if k % 512:
        return np.exp2(np.random.permutation(np.resize(levels, k // 32))).repeat(32)
    a = np.empty((k // 512, 16))
    for p in range(k // 512):
        a[p, :8] = np.random.permutation(np.resize(levels, 8))
        for g in range(8):
            far = levels[np.abs(levels - a[p, g]) >= 10]
            a[p, g + 8] = far[np.random.randint(len(far))]
    return np.exp2(a.ravel()).repeat(32)


BF16 = ml_dtypes.bfloat16


def bf(x):
    return np.asarray(x, np.float32).astype(BF16)


def f64(x):
    return np.asarray(x).astype(np.float64)


E2M1 = np.array([0.0, 0.5, 1.0, 1.5, 2.0, 3.0, 4.0, 6.0, -0.0, -0.5, -1.0, -1.5, -2.0, -3.0, -4.0, -6.0])


def pack_weight(w, fmt):
    k, n = w.shape
    w = f64(bf(w)).reshape(k // 32, 32, n)
    amax = np.abs(w).max(1)
    if fmt == "e4m3":
        byte = np.frexp(amax)[1] - 1 + 127 - 7
    else:
        mant, ex = np.frexp(amax / 6.0)
        byte = np.where(mant > 0.5, ex, ex - 1) + 127
    byte = np.clip(np.where(amax > 0, byte, 1), 1, 254)
    scaled = (w * np.exp2(127.0 - byte)[:, None, :]).reshape(k, n).astype(np.float32)
    by_word = np.ascontiguousarray(scaled.reshape(k // 512, 128, 4, n).transpose(0, 1, 3, 2))
    if fmt == "e4m3":
        words = by_word.astype(ml_dtypes.float8_e4m3fn).view(np.uint8)
    else:
        c = by_word.astype(ml_dtypes.float4_e2m1fn).view(np.uint8) & 0xF
        words = c[..., 0::2] | (c[..., 1::2] << 4)
    return np.ascontiguousarray(words), np.ascontiguousarray(byte.astype(np.uint8).reshape(k // 512, 16, n))


def unpack_weight(words, scales, fmt):
    g, p, n, _ = words.shape
    if fmt == "e4m3":
        vals = np.ascontiguousarray(words).view(ml_dtypes.float8_e4m3fn).astype(np.float64)
    else:
        nib = np.empty((g, p, n, 4), np.uint8)
        nib[..., 0::2] = words & 0xF
        nib[..., 1::2] = words >> 4
        vals = E2M1[nib]
    vals = vals * np.repeat(np.exp2(scales.astype(np.float64) - 127.0), 8, axis=1)[..., None]
    return vals.transpose(0, 1, 3, 2).reshape(g * 512, n)
def pack4(w):
    words, scales = pack_weight(w, "e2m1")
    return words.reshape(words.shape[0], 128, -1), scales


def unpack4(words, scales):
    return unpack_weight(words.reshape(words.shape[0], 128, -1, 2), scales, "e2m1")


E4M3FN = np.array([(-1.0 if i & 128 else 1.0) * ((1.0 + (i & 7) / 8.0) * 2.0 ** (((i >> 3) & 15) - 7) if i & 120 else (i & 7) * 2.0 ** -9) for i in range(256)])


def e4m3fn_bytes(y):
    return np.clip(np.asarray(y, np.float64), -448.0, 448.0).astype(np.float32).astype(ml_dtypes.float8_e4m3fn).view(np.uint8)


def e4m3fn_values(b):
    return E4M3FN[b]

def planes(Y):
    n, m = Y.shape
    b = f64(bf(Y)).reshape(n // 32, 32, m)
    amax = np.abs(b).max(1)
    byte = np.clip(np.where(amax > 0, np.frexp(amax)[1] - 1 + 127 - 7, 1), 1, 254)
    codes = (b * np.exp2(127.0 - byte)[:, None, :]).reshape(n, m).astype(np.float32).astype(ml_dtypes.float8_e4m3fn).view(np.uint8)
    words = codes.reshape(n // 512, 128, 4, m).transpose(0, 1, 3, 2)
    return np.ascontiguousarray(words), np.ascontiguousarray(byte.astype(np.uint8).reshape(n // 512, 16, m))


T, K, N, B = 1024, 1536, 1536, 128
GAMMA = 0.9
STEPS = 5
FP8_MAX = 448.0

def setup_inputs():
    s = mx_kscale(K)[:, None]
    F = np.random.randn(K, T) * s
    F_words, F_scales = pack_weight(F, "e4m3")
    size = np.exp(0.8 * np.random.randn(1, N))
    common = 0.8 * np.random.randn(K, N)
    W1 = (common + 0.6 * np.random.randn(K, N)) * size / np.sqrt(K) / s
    W2 = (common + 0.6 * np.random.randn(K, N)) * size / np.sqrt(K) / s
    W1_scale = np.float32(np.abs(W1).reshape(K // B, B, N // B, B).max(axis=(1, 3)) / FP8_MAX)
    W1_bytes = e4m3fn_bytes(W1 / np.repeat(np.repeat(f64(W1_scale), B, axis=0), B, axis=1))
    W2_words, W2_scales = pack4(W2)
    return {"F_words": F_words, "F_scales": F_scales,
            "W1_bytes": W1_bytes, "W1_scale": W1_scale,
            "W2_words": W2_words, "W2_scales": W2_scales,
            "b1": bf(0.3 * np.random.randn(1, N) * size),
            "b2": bf(0.3 * np.random.randn(1, N) * size),
            "disc": bf(GAMMA ** np.random.randint(1, STEPS + 1, size=(T, 1))),
            "reward": bf(0.8 * np.random.randn(T, N) * size)}

def reference(F_words, F_scales, W1_bytes, W1_scale, W2_words, W2_scales, b1, b2, disc, reward):
    F = unpack_weight(F_words, F_scales, "e4m3")
    W1 = e4m3fn_values(W1_bytes) * np.repeat(np.repeat(f64(W1_scale), B, axis=0), B, axis=1)
    W2 = unpack4(W2_words, W2_scales)
    q1 = (F.T @ mxq(W1, 0, "e4m3")) + f64(b1)
    q2 = (F.T @ W2) + f64(b2)
    y = f64(reward) + f64(disc) * np.minimum(q1, q2)
    words, scales = planes(y.T)
    return y, words, scales

@@ -1,0 +1,344 @@
+from contextlib import ExitStack
+
+import concourse.mybir as mybir
+from concourse.masks import make_identity
+
+T, K, N = 1024, 1536, 1536
+FLOPS = 2 * 2 * T * K * N
+
+F32 = mybir.dt.float32
+BF16 = mybir.dt.bfloat16
+I32 = mybir.dt.int32
+U32 = mybir.dt.uint32
+U8 = mybir.dt.uint8
+FP8 = mybir.dt.float8_e4m3fn
+FP8X4 = mybir.dt.float8_e4m3fn_x4
+FP4X4 = mybir.dt.float4_e2m1fn_x4
+ALU = mybir.AluOpType
+ACT = mybir.ActivationFunctionType
+
+P = 128
+W = 512
+PASSES = K // W
+GROUPS = N // W
+HALVES = T // W
+TILES = W // P
+BLOCKS = GROUPS * HALVES * TILES
+LEAD = 8
+
+
+def tile_twin_critic_bellman_targets_b7_kernel(
+    tc, F_words, F_scales, W1_bytes, W1_scale, W2_words, W2_scales, b1, b2, disc, reward, out_0, out_1, out_2
+):
+    nc = tc.nc
+    with ExitStack() as ctx:
+        keep = ctx.enter_context(tc.tile_pool(name="keep", bufs=1))
+        work = ctx.enter_context(tc.tile_pool(name="work", bufs=2))
+        psum = ctx.enter_context(tc.psum_pool(name="psum", bufs=1))
+        ctx.enter_context(tc.manual_schedule())
+
+        def bank(b):
+            return psum.tile([P, W], F32, name=f"bank{b}")
+
+        f_sc = keep.tile([P, PASSES, T], U8, name="f_sc", align_bytes=64)
+        w2_sc0 = keep.tile([P, PASSES, W], U8, name="w2_sc0", align_bytes=64)
+        w2_sc1 = keep.tile([P, PASSES, N - W], U8, name="w2_sc1", align_bytes=64)
+        rows32 = keep.tile([P, P], F32, name="rows32")
+        rows16 = keep.tile([32, P], BF16, name="rows16")
+        cols = keep.tile([P, 32], F32, name="cols")
+        s_all = keep.tile([P, 144], F32, name="s_all")
+        w1_s = keep.tile([P, PASSES * 12], F32, name="w1_s")
+        ident = keep.tile([P, P], F32, name="ident")
+
+        for t in (f_sc, w2_sc0, w2_sc1):
+            nc.vector.memset(t[:].rearrange("p c n -> p (c n)").bitcast(I32), 0)
+        nc.vector.memset(rows32[:], 0.0)
+
+        make_identity(nc, ident[:])
+        nc.gpsimd.dma_start(out=rows16[12:24, :], in_=b2.rearrange("o (a p) -> (o a) p", p=P))
+        nc.gpsimd.dma_start(out=rows16[0:12, :], in_=b1.rearrange("o (a p) -> (o a) p", p=P))
+        nc.gpsimd.dma_start(out=rows16[24:32, :], in_=disc.rearrange("(a p) o -> a (p o)", p=P))
+
+        f_codes, w2_codes, w1_raw, rew = {}, {}, {}, {}
+
+        def load_f(c, h):
+            t = keep.tile([P, W], U32, name=f"f_codes{c}{h}", align_bytes=64)
+            src = F_words[c].rearrange("p n t -> p (n t)")[:, 4 * W * h : 4 * W * (h + 1)]
+            nc.sync.dma_start(out=t[:].bitcast(I32), in_=src.bitcast(I32))
+            f_codes[c, h] = t
+
+        def load_w2(g):
+            t = keep.tile([P, PASSES, 2 * W], U8, name=f"w2_codes{g}", align_bytes=64)
+            src = W2_words[:, :, 2 * W * g : 2 * W * (g + 1)].rearrange("c p n -> p c n")
+            nc.sync.dma_start(out=t[:].bitcast(I32), in_=src.bitcast(I32))
+            w2_codes[g] = t
+
+        def load_scales(t, dram, lo, hi):
+            for q in range(4):
+                src = dram[:, 4 * q : 4 * q + 4, lo:hi].rearrange("c r n -> r c n")
+                nc.sync.dma_start(out=t[32 * q : 32 * q + 4, :, :].bitcast(I32), in_=src.bitcast(I32))
+
+        def load_w1(g, c):
+            t = keep.tile([P, 4, W], U8, name=f"w1_raw{g}{c}")
+            src = W1_bytes[W * c : W * (c + 1), W * g : W * (g + 1)].rearrange("(p t) n -> p t n", t=4)
+            nc.sync.dma_start(out=t[:], in_=src)
+            w1_raw[g, c] = t
+
+        def load_reward(g, h):
+            t = keep.tile([P, TILES, W], BF16, name=f"rew{g}{h}")
+            src = reward[W * h : W * (h + 1), W * g : W * (g + 1)].rearrange("(i p) n -> p i n", p=P)
+            nc.sync.dma_start(out=t[:], in_=src)
+            rew[g, h] = t
+
+        load_f(0, 0)
+        load_w2(0)
+        load_scales(f_sc, F_scales, 0, T)
+        load_scales(w2_sc0, W2_scales, 0, W)
+        load_f(1, 0)
+        load_f(2, 0)
+        nc.sync.dma_start(out=s_all[:], in_=W1_scale.rearrange("a b -> (a b)").partition_broadcast(P))
+        for c in range(PASSES):
+            load_w1(0, c)
+        for c in range(PASSES):
+            load_f(c, 1)
+        load_w2(1)
+        load_scales(w2_sc1, W2_scales, W, N)
+        for c in range(PASSES):
+            load_w1(1, c)
+        load_reward(0, 0)
+        load_w2(2)
+        load_reward(0, 1)
+        for c in range(PASSES):
+            load_w1(2, c)
+        for g in range(1, GROUPS):
+            for h in range(HALVES):
+                load_reward(g, h)
+
+        def place(k):
+            return k // (HALVES * TILES), (k // TILES) % HALVES, k % TILES
+
+        w1_codes, w1_sc, wide, inter, q2_bank, a2, m = {}, {}, {}, {}, {}, {}, {}
+        for jj in range(GROUPS * TILES):
+            w1_codes[jj] = keep.tile([P, PASSES, P], U32, name=f"w1_codes{jj}", align_bytes=64)
+            w1_sc[jj] = keep.tile([P, PASSES, P], U8, name=f"w1_sc{jj}", align_bytes=64)
+
+        def mm_q2(k, b):
+            g, h, j = place(k)
+            acc = bank(b)
+            sc, lo = (w2_sc0, P * j) if g == 0 else (w2_sc1, W * (g - 1) + P * j)
+            for c in range(PASSES):
+                nc.tensor.matmul_mx(
+                    out=acc[:],
+                    lhsT=w2_codes[g][:, c, 2 * P * j : 2 * P * (j + 1)].bitcast(FP4X4),
+                    lhsT_scale=sc[:, c, lo : lo + P],
+                    rhs=f_codes[c, h][:].bitcast(FP8X4),
+                    rhs_scale=f_sc[:, c, W * h : W * (h + 1)],
+                    start=(c == 0),
+                    stop=(c == PASSES - 1),
+                )
+            q2_bank[k] = acc
+
+        def bias_q2(k, on_vector=False):
+            g, h, j = place(k)
+            t = work.tile([P, W], F32, name="a2", bufs=LEAD + 2)
+            col = cols[:, 12 + TILES * g + j : 13 + TILES * g + j]
+            if on_vector:
+                nc.vector.tensor_scalar(out=t[:], in0=q2_bank[k][:], scalar1=col, scalar2=None, op0=ALU.add)
+            else:
+                nc.scalar.activation(out=t[:], in_=q2_bank[k][:], func=ACT.Identity, bias=col)
+            a2[k] = t
+
+        def mm_q1(k, b):
+            g, h, j = place(k)
+            jj = TILES * g + j
+            acc = bank(b)
+            for c in range(PASSES):
+                nc.tensor.matmul_mx(
+                    out=acc[:],
+                    lhsT=w1_codes[jj][:, c, :].bitcast(FP8X4),
+                    lhsT_scale=w1_sc[jj][:, c, :],
+                    rhs=f_codes[c, h][:].bitcast(FP8X4),
+                    rhs_scale=f_sc[:, c, W * h : W * (h + 1)],
+                    start=(c == 0),
+                    stop=(c == PASSES - 1),
+                )
+            return acc
+
+        def take_min(k, acc):
+            g, h, j = place(k)
+            t = work.tile([P, W], F32, name="m", bufs=2 * TILES)
+            col = cols[:, TILES * g + j : TILES * g + j + 1]
+            nc.vector.scalar_tensor_tensor(out=t[:], in0=acc[:], scalar=col, in1=a2[k][:], op0=ALU.add, op1=ALU.min)
+            m[k] = t
+
+        def widen(g, c, on_vector=False):
+            t = work.tile([P, 4 * W], BF16, name="wide", bufs=4)
+            src = w1_raw[g, c][:].rearrange("p t n -> p (t n)").bitcast(FP8)
+            if on_vector:
+                nc.vector.tensor_copy(out=t[:], in_=src)
+            else:
+                nc.scalar.copy(out=t[:], in_=src)
+            wide[g, c] = t
+
+        pieces = [(0, c, j) for j in range(TILES) for c in range(PASSES)]
+        pieces = pieces + [(g, c, j) for g in range(1, GROUPS) for c in range(PASSES) for j in range(TILES)]
+
+        def quantize_piece(n):
+            g, c, j = pieces[n]
+            jj = TILES * g + j
+            nc.vector.quantize_mx(out=w1_codes[jj][:, c, :].bitcast(FP8X4), scales=w1_sc[jj][:, c, :], in_=inter[n][:])
+
+        def prep(n):
+            if n < len(pieces):
+                g, c, j = pieces[n]
+                t = work.tile([P, W], BF16, name="inter", bufs=3, align_bytes=64)
+                src = wide[g, c][:].rearrange("p (t n) -> p t n", t=4)[:, :, P * j : P * (j + 1)]
+                col = w1_s[:, 12 * c + TILES * g + j : 12 * c + TILES * g + j + 1]
+                nc.vector.tensor_scalar(
+                    out=t[:].rearrange("p (a i t) -> p a t i", i=4, t=4),
+                    in0=src.rearrange("p t (a i) -> p a t i", i=4),
+                    scalar1=col,
+                    scalar2=None,
+                    op0=ALU.mult,
+                )
+                inter[n] = t
+            if 0 < n <= len(pieces):
+                quantize_piece(n - 1)
+
+        mt_bank, word_bank, y, yb, grouped, y_codes, y_sc = {}, {}, {}, {}, {}, {}, {}
+
+        def turn_min(r, banks):
+            u, pair = divmod(r, 2)
+            for ii in range(2):
+                i = 2 * pair + ii
+                acc = bank(banks[ii])
+                for j in range(TILES):
+                    nc.tensor.transpose(acc[:, P * j : P * (j + 1)], m[TILES * u + j][:, P * i : P * (i + 1)], ident[:])
+                mt_bank[r, ii] = acc
+
+        def make_y(r, ii):
+            u, pair = divmod(r, 2)
+            g, h = divmod(u, HALVES)
+            i = 2 * pair + ii
+            t = work.tile([P, W], F32, name="y", bufs=4)
+            col = cols[:, 24 + TILES * h + i : 25 + TILES * h + i]
+            nc.vector.scalar_tensor_tensor(
+                out=t[:], in0=mt_bank[r, ii][:], scalar=col, in1=rew[g, h][:, i, :], op0=ALU.mult, op1=ALU.add
+            )
+            row = W * h + P * i
+            nc.sync.dma_start(out=out_0[row : row + P, W * g : W * (g + 1)], in_=t[:])
+            y[r, ii] = t
+
+        def round_y(r, ii):
+            t = work.tile([P, W], BF16, name="yb", bufs=4)
+            nc.scalar.copy(
+                out=t[:].rearrange("r (u p e) -> r u p e", u=2, e=2),
+                in_=y[r, ii][:].rearrange("r (p u e) -> r u p e", u=2, e=2),
+            )
+            yb[r, ii] = t
+
+        def turn_words(r):
+            acc = bank(6 + r % 2)
+            for ii in range(2):
+                words = yb[r, ii][:].bitcast(F32)
+                for u in range(2):
+                    lo = 2 * P * ii + P * u
+                    nc.tensor.transpose(acc[:, lo : lo + P], words[:, P * u : P * (u + 1)], ident[:])
+            word_bank[r] = acc
+
+        def group_words(r):
+            t = work.tile([P, 2 * W], BF16, name="grouped", bufs=2, align_bytes=64)
+            nc.scalar.copy(
+                out=t[:].bitcast(F32).rearrange("p (i r u) -> p i r u", i=2, u=2),
+                in_=word_bank[r][:].rearrange("p (i u r) -> p i r u", i=2, u=2),
+            )
+            grouped[r] = t
+
+        def quantize_y(r):
+            u, pair = divmod(r, 2)
+            g, h = divmod(u, HALVES)
+            if h == 0 and pair == 0:
+                y_sc[g] = work.tile([P, T], U8, name="y_sc", bufs=2, align_bytes=64)
+            t = work.tile([P, 2 * P], U32, name="y_codes", bufs=3, align_bytes=64)
+            lo = W * h + 2 * P * pair
+            nc.vector.quantize_mx(out=t[:].bitcast(FP8X4), scales=y_sc[g][:, lo : lo + 2 * P], in_=grouped[r][:])
+            dst = out_1[g].rearrange("p n t -> p (n t)")[:, 4 * lo : 4 * (lo + 2 * P)]
+            nc.sync.dma_start(out=dst.bitcast(I32), in_=t[:].bitcast(I32))
+            if h == HALVES - 1 and pair == 1:
+                for q in range(4):
+                    nc.sync.dma_start(
+                        out=out_2[g, 4 * q : 4 * q + 4, :].bitcast(I32), in_=y_sc[g][32 * q : 32 * q + 4, :].bitcast(I32)
+                    )
+
+        nc.scalar.activation(out=rows32[0:32, :], in_=rows16[:], func=ACT.Identity)
+        for k in range(3):
+            mm_q2(k, k)
+        cb = bank(7)
+        nc.tensor.transpose(cb[:, 0:P], rows32[:], ident[:])
+        for q in range(4):
+            nc.vector.tensor_copy(
+                out=w1_s[32 * q : 32 * q + 32, :].rearrange("p (c j) -> p c j", c=PASSES),
+                in_=s_all[32 * q : 32 * q + 32, :].rearrange("p (c q j) -> p c q j", c=PASSES, q=4)[:, :, q, :],
+            )
+        nc.vector.tensor_copy(out=cols[:], in_=cb[:, 0:32])
+        for k in range(3, LEAD):
+            mm_q2(k, k)
+        bias_q2(0)
+        bias_q2(1)
+        widen(0, 0)
+        widen(0, 1)
+        bias_q2(2, on_vector=True)
+        widen(0, 2, on_vector=True)
+        for k in range(3, LEAD):
+            bias_q2(k)
+        for n in range(7):
+            prep(n)
+        done = 7
+
+        for k in range(BLOCKS):
+            r = (k - TILES) // 2
+            if k + LEAD < BLOCKS:
+                mm_q2(k + LEAD, k % 2)
+                bias_q2(k + LEAD)
+            if k % 2 == 1 and r >= 0:
+                round_y(r, 1)
+            if k % 2 == 0 and k // 2 < 2 * PASSES:
+                widen(1 + k // (2 * PASSES), (k // 2) % PASSES)
+            count = 3 if k < 2 else 2
+            prep(done)
+            if k % 2 == 1 and r >= 1:
+                quantize_y(r - 1)
+            for n in range(done + 1, done + count):
+                prep(n)
+            done = done + count
+            take_min(k, mm_q1(k, 2 + k % 2))
+            if k % 2 == 0 and r >= 0:
+                turn_min(r, (4, 5))
+                if r >= 1:
+                    turn_words(r - 1)
+                make_y(r, 0)
+                make_y(r, 1)
+                if r >= 1:
+                    group_words(r - 1)
+                round_y(r, 0)
+
+        last = BLOCKS // 2 - 1
+        turn_min(last - 1, (4, 5))
+        turn_min(last, (0, 1))
+        turn_words(last - 2)
+        make_y(last - 1, 0)
+        make_y(last - 1, 1)
+        group_words(last - 2)
+        round_y(last - 1, 0)
+        round_y(last - 1, 1)
+        make_y(last, 0)
+        quantize_y(last - 2)
+        make_y(last, 1)
+        turn_words(last - 1)
+        round_y(last, 0)
+        group_words(last - 1)
+        round_y(last, 1)
+        quantize_y(last - 1)
+        turn_words(last)
+        group_words(last)
+        quantize_y(last)

@@ -25,6 +25,11 @@ HALVES = T // W
 TILES = W // P
 BLOCKS = GROUPS * HALVES * TILES
 LEAD = 8
+HEAD_PIECES = 7
+HEAD_V = 2
+EAGER = 2
+AHEAD = 2
+SKIP = ()
 
 
 def tile_twin_critic_bellman_targets_b7_kernel(
@@ -54,10 +59,11 @@ def tile_twin_critic_bellman_targets_b7_kernel(
             nc.vector.memset(t[:].rearrange("p c n -> p (c n)").bitcast(I32), 0)
         nc.vector.memset(rows32[:], 0.0)
 
-        make_identity(nc, ident[:])
         nc.gpsimd.dma_start(out=rows16[12:24, :], in_=b2.rearrange("o (a p) -> (o a) p", p=P))
         nc.gpsimd.dma_start(out=rows16[0:12, :], in_=b1.rearrange("o (a p) -> (o a) p", p=P))
         nc.gpsimd.dma_start(out=rows16[24:32, :], in_=disc.rearrange("(a p) o -> a (p o)", p=P))
+
+        make_identity(nc, ident[:])
 
         f_codes, w2_codes, w1_raw, rew = {}, {}, {}, {}
 
@@ -148,37 +154,43 @@ def tile_twin_critic_bellman_targets_b7_kernel(
                 nc.scalar.activation(out=t[:], in_=q2_bank[k][:], func=ACT.Identity, bias=col)
             a2[k] = t
 
-        def mm_q1(k, b):
+        def mm_q1(k, acc, lo=0, hi=W):
             g, h, j = place(k)
             jj = TILES * g + j
-            acc = bank(b)
             for c in range(PASSES):
                 nc.tensor.matmul_mx(
-                    out=acc[:],
+                    out=acc,
                     lhsT=w1_codes[jj][:, c, :].bitcast(FP8X4),
                     lhsT_scale=w1_sc[jj][:, c, :],
-                    rhs=f_codes[c, h][:].bitcast(FP8X4),
-                    rhs_scale=f_sc[:, c, W * h : W * (h + 1)],
+                    rhs=f_codes[c, h][:, lo:hi].bitcast(FP8X4),
+                    rhs_scale=f_sc[:, c, W * h + lo : W * h + hi],
                     start=(c == 0),
                     stop=(c == PASSES - 1),
                 )
             return acc
 
-        def take_min(k, acc):
+        def take_min(k, acc, lo=0, hi=W):
             g, h, j = place(k)
-            t = work.tile([P, W], F32, name="m", bufs=2 * TILES)
-            col = cols[:, TILES * g + j : TILES * g + j + 1]
-            nc.vector.scalar_tensor_tensor(out=t[:], in0=acc[:], scalar=col, in1=a2[k][:], op0=ALU.add, op1=ALU.min)
-            m[k] = t
-
-        def widen(g, c, on_vector=False):
-            t = work.tile([P, 4 * W], BF16, name="wide", bufs=4)
-            src = w1_raw[g, c][:].rearrange("p t n -> p (t n)").bitcast(FP8)
-            if on_vector:
-                nc.vector.tensor_copy(out=t[:], in_=src)
+            if hi - lo == W:
+                t = work.tile([P, W], F32, name="m", bufs=2 * TILES)
             else:
-                nc.scalar.copy(out=t[:], in_=src)
-            wide[g, c] = t
+                t = work.tile([P, hi - lo], F32, name="m_last", bufs=2 * TILES)
+            col = cols[:, TILES * g + j : TILES * g + j + 1]
+            nc.vector.scalar_tensor_tensor(
+                out=t[:], in0=acc, scalar=col, in1=a2[k][:, lo:hi], op0=ALU.add, op1=ALU.min
+            )
+            for i in range(lo // P, hi // P):
+                m[k, i] = t[:, P * i - lo : P * (i + 1) - lo]
+
+        def widen(g, c, half, on_vector=False):
+            if half == 0:
+                wide[g, c] = work.tile([P, 4 * W], BF16, name="wide", bufs=4)
+            lo, hi = 2 * W * half, 2 * W * (half + 1)
+            src = w1_raw[g, c][:].rearrange("p t n -> p (t n)")[:, lo:hi].bitcast(FP8)
+            if on_vector:
+                nc.vector.tensor_copy(out=wide[g, c][:, lo:hi], in_=src)
+            else:
+                nc.scalar.copy(out=wide[g, c][:, lo:hi], in_=src)
 
         pieces = [(0, c, j) for j in range(TILES) for c in range(PASSES)]
         pieces = pieces + [(g, c, j) for g in range(1, GROUPS) for c in range(PASSES) for j in range(TILES)]
@@ -205,74 +217,72 @@ def tile_twin_critic_bellman_targets_b7_kernel(
             if 0 < n <= len(pieces):
                 quantize_piece(n - 1)
 
-        mt_bank, word_bank, y, yb, grouped, y_codes, y_sc = {}, {}, {}, {}, {}, {}, {}
+        mt_bank, word_bank, y, yb, grouped, y_sc = {}, {}, {}, {}, {}, {}
 
-        def turn_min(r, banks):
-            u, pair = divmod(r, 2)
-            for ii in range(2):
-                i = 2 * pair + ii
-                acc = bank(banks[ii])
-                for j in range(TILES):
-                    nc.tensor.transpose(acc[:, P * j : P * (j + 1)], m[TILES * u + j][:, P * i : P * (i + 1)], ident[:])
-                mt_bank[r, ii] = acc
+        def turn_min(x, b):
+            u, i = divmod(x, TILES)
+            acc = bank(b)
+            for j in range(TILES):
+                nc.tensor.transpose(acc[:, P * j : P * (j + 1)], m[TILES * u + j, i], ident[:])
+            mt_bank[x] = acc
 
-        def make_y(r, ii):
-            u, pair = divmod(r, 2)
+        def make_y(x):
+            u, i = divmod(x, TILES)
             g, h = divmod(u, HALVES)
-            i = 2 * pair + ii
-            t = work.tile([P, W], F32, name="y", bufs=4)
+            t = work.tile([P, W], F32, name="y", bufs=6)
             col = cols[:, 24 + TILES * h + i : 25 + TILES * h + i]
             nc.vector.scalar_tensor_tensor(
-                out=t[:], in0=mt_bank[r, ii][:], scalar=col, in1=rew[g, h][:, i, :], op0=ALU.mult, op1=ALU.add
+                out=t[:], in0=mt_bank[x][:], scalar=col, in1=rew[g, h][:, i, :], op0=ALU.mult, op1=ALU.add
             )
             row = W * h + P * i
             nc.sync.dma_start(out=out_0[row : row + P, W * g : W * (g + 1)], in_=t[:])
-            y[r, ii] = t
+            y[x] = t
 
-        def round_y(r, ii):
-            t = work.tile([P, W], BF16, name="yb", bufs=4)
+        def round_y(x, on_vector=False):
+            t = work.tile([P, W], BF16, name="yb", bufs=6)
+            dst = t[:].rearrange("r (u p e) -> r u p e", u=2, e=2)
+            src = y[x][:].rearrange("r (p u e) -> r u p e", u=2, e=2)
+            if on_vector:
+                nc.vector.tensor_copy(out=dst, in_=src)
+            else:
+                nc.scalar.copy(out=dst, in_=src)
+            yb[x] = t
+
+        def turn_words(x, n, b):
+            acc = bank(b)
+            for ii in range(n):
+                words = yb[x + ii][:].bitcast(F32)
+                for v in range(2):
+                    lo = 2 * P * ii + P * v
+                    nc.tensor.transpose(acc[:, lo : lo + P], words[:, P * v : P * (v + 1)], ident[:])
+            word_bank[x] = acc
+
+        def group_words(x, n):
+            t = work.tile([P, n * W], BF16, name="grouped", bufs=5, align_bytes=64)
             nc.scalar.copy(
-                out=t[:].rearrange("r (u p e) -> r u p e", u=2, e=2),
-                in_=y[r, ii][:].rearrange("r (p u e) -> r u p e", u=2, e=2),
+                out=t[:].bitcast(F32).rearrange("p (i r u) -> p i r u", i=n, u=2),
+                in_=word_bank[x][:, 0 : 2 * P * n].rearrange("p (i u r) -> p i r u", i=n, u=2),
             )
-            yb[r, ii] = t
+            grouped[x] = t
 
-        def turn_words(r):
-            acc = bank(6 + r % 2)
-            for ii in range(2):
-                words = yb[r, ii][:].bitcast(F32)
-                for u in range(2):
-                    lo = 2 * P * ii + P * u
-                    nc.tensor.transpose(acc[:, lo : lo + P], words[:, P * u : P * (u + 1)], ident[:])
-            word_bank[r] = acc
-
-        def group_words(r):
-            t = work.tile([P, 2 * W], BF16, name="grouped", bufs=2, align_bytes=64)
-            nc.scalar.copy(
-                out=t[:].bitcast(F32).rearrange("p (i r u) -> p i r u", i=2, u=2),
-                in_=word_bank[r][:].rearrange("p (i u r) -> p i r u", i=2, u=2),
-            )
-            grouped[r] = t
-
-        def quantize_y(r):
-            u, pair = divmod(r, 2)
+        def quantize_y(x, n):
+            u, i = divmod(x, TILES)
             g, h = divmod(u, HALVES)
-            if h == 0 and pair == 0:
+            if h == 0 and i == 0:
                 y_sc[g] = work.tile([P, T], U8, name="y_sc", bufs=2, align_bytes=64)
-            t = work.tile([P, 2 * P], U32, name="y_codes", bufs=3, align_bytes=64)
-            lo = W * h + 2 * P * pair
-            nc.vector.quantize_mx(out=t[:].bitcast(FP8X4), scales=y_sc[g][:, lo : lo + 2 * P], in_=grouped[r][:])
-            dst = out_1[g].rearrange("p n t -> p (n t)")[:, 4 * lo : 4 * (lo + 2 * P)]
+            t = work.tile([P, n * P], U32, name="y_codes", bufs=6, align_bytes=64)
+            lo = W * h + P * i
+            nc.vector.quantize_mx(out=t[:].bitcast(FP8X4), scales=y_sc[g][:, lo : lo + n * P], in_=grouped[x][:])
+            dst = out_1[g].rearrange("p n t -> p (n t)")[:, 4 * lo : 4 * (lo + n * P)]
             nc.sync.dma_start(out=dst.bitcast(I32), in_=t[:].bitcast(I32))
-            if h == HALVES - 1 and pair == 1:
+            if lo + n * P == T:
                 for q in range(4):
                     nc.sync.dma_start(
                         out=out_2[g, 4 * q : 4 * q + 4, :].bitcast(I32), in_=y_sc[g][32 * q : 32 * q + 4, :].bitcast(I32)
                     )
 
         nc.scalar.activation(out=rows32[0:32, :], in_=rows16[:], func=ACT.Identity)
-        for k in range(3):
-            mm_q2(k, k)
+        mm_q2(0, 0)
         cb = bank(7)
         nc.tensor.transpose(cb[:, 0:P], rows32[:], ident[:])
         for q in range(4):
@@ -281,64 +291,114 @@ def tile_twin_critic_bellman_targets_b7_kernel(
                 in_=s_all[32 * q : 32 * q + 32, :].rearrange("p (c q j) -> p c q j", c=PASSES, q=4)[:, :, q, :],
             )
         nc.vector.tensor_copy(out=cols[:], in_=cb[:, 0:32])
-        for k in range(3, LEAD):
+        for k in range(1, LEAD):
             mm_q2(k, k)
-        bias_q2(0)
-        bias_q2(1)
-        widen(0, 0)
-        widen(0, 1)
-        bias_q2(2, on_vector=True)
-        widen(0, 2, on_vector=True)
-        for k in range(3, LEAD):
+        for c in range(PASSES):
+            widen(0, c, 0, on_vector=True)
+            widen(0, c, 1, on_vector=(c == HEAD_V))
+        for k in range(LEAD):
             bias_q2(k)
-        for n in range(7):
+        for n in range(HEAD_PIECES):
             prep(n)
-        done = 7
-
+        done = HEAD_PIECES
+        next_q2 = LEAD
+        counts = [3 if k < EAGER else 2 for k in range(BLOCKS)]
+        first_use = {}
+        n = done
         for k in range(BLOCKS):
-            r = (k - TILES) // 2
-            if k + LEAD < BLOCKS:
-                mm_q2(k + LEAD, k % 2)
-                bias_q2(k + LEAD)
-            if k % 2 == 1 and r >= 0:
-                round_y(r, 1)
-            if k % 2 == 0 and k // 2 < 2 * PASSES:
-                widen(1 + k // (2 * PASSES), (k // 2) % PASSES)
-            count = 3 if k < 2 else 2
-            prep(done)
-            if k % 2 == 1 and r >= 1:
-                quantize_y(r - 1)
-            for n in range(done + 1, done + count):
-                prep(n)
-            done = done + count
-            take_min(k, mm_q1(k, 2 + k % 2))
-            if k % 2 == 0 and r >= 0:
-                turn_min(r, (4, 5))
-                if r >= 1:
-                    turn_words(r - 1)
-                make_y(r, 0)
-                make_y(r, 1)
-                if r >= 1:
-                    group_words(r - 1)
-                round_y(r, 0)
+            for g, c, j in pieces[n : n + counts[k]]:
+                first_use.setdefault((g, c), k)
+            n = n + counts[k]
 
-        last = BLOCKS // 2 - 1
-        turn_min(last - 1, (4, 5))
-        turn_min(last, (0, 1))
-        turn_words(last - 2)
-        make_y(last - 1, 0)
-        make_y(last - 1, 1)
-        group_words(last - 2)
-        round_y(last - 1, 0)
-        round_y(last - 1, 1)
-        make_y(last, 0)
-        quantize_y(last - 2)
-        make_y(last, 1)
-        turn_words(last - 1)
-        round_y(last, 0)
-        group_words(last - 1)
-        round_y(last, 1)
-        quantize_y(last - 1)
-        turn_words(last)
-        group_words(last)
-        quantize_y(last)
+        for k in range(BLOCKS - TILES):
+            x = 2 * ((k - TILES) // 2)
+            if next_q2 < BLOCKS and k not in SKIP:
+                mm_q2(next_q2, next_q2 % 2)
+                bias_q2(next_q2)
+                next_q2 = next_q2 + 1
+            if k % 2 == 1 and x >= 0:
+                round_y(x + 1)
+            for g in range(1, GROUPS):
+                for c in range(PASSES):
+                    for half in range(2):
+                        if k == max(0, first_use[g, c] - AHEAD + half):
+                            widen(g, c, half)
+            count = counts[k]
+            for n in range(done, done + count):
+                prep(n)
+            if k % 2 == 1 and x >= 2:
+                quantize_y(x - 2, 2)
+            done = done + count
+            take_min(k, mm_q1(k, bank(2 + k % 2)[:]))
+            if k % 2 == 0 and x >= 0:
+                turn_min(x, 4)
+                turn_min(x + 1, 5)
+                if x >= 2:
+                    turn_words(x - 2, 2, 6 + (x // 2) % 2)
+                make_y(x)
+                make_y(x + 1)
+                if x >= 2:
+                    group_words(x - 2, 2)
+                round_y(x)
+
+        last_bank = {}
+
+        def last_mm(i):
+            last_bank[i] = bank(i % 2)
+            for j in range(TILES):
+                mm_q1(BLOCKS - TILES + j, last_bank[i][:, P * j : P * (j + 1)], P * i, P * (i + 1))
+
+        def last_min(i):
+            for j in range(TILES):
+                take_min(BLOCKS - TILES + j, last_bank[i][:, P * j : P * (j + 1)], P * i, P * (i + 1))
+
+        last_mm(0)
+        turn_min(16, 4)
+        turn_min(17, 5)
+        turn_words(14, 2, 6)
+        turn_min(18, 2)
+        turn_min(19, 3)
+        last_mm(1)
+        last_min(0)
+        make_y(16)
+        make_y(17)
+        group_words(14, 2)
+        round_y(16)
+        round_y(17)
+        make_y(18)
+        last_min(1)
+        last_mm(2)
+        turn_min(20, 4)
+        turn_words(16, 2, 7)
+        turn_min(21, 5)
+        last_mm(3)
+        make_y(19)
+        round_y(18)
+        round_y(19)
+        group_words(16, 2)
+        last_min(2)
+        quantize_y(14, 2)
+        make_y(20)
+        round_y(20)
+        last_min(3)
+        turn_min(22, 2)
+        turn_words(18, 2, 6)
+        turn_min(23, 3)
+        make_y(21)
+        group_words(18, 2)
+        round_y(21)
+        make_y(22)
+        turn_words(20, 2, 7)
+        round_y(22)
+        make_y(23)
+        group_words(20, 2)
+        quantize_y(16, 2)
+        round_y(23, on_vector=True)
+        turn_words(22, 1, 0)
+        turn_words(23, 1, 1)
+        quantize_y(18, 2)
+        group_words(22, 1)
+        quantize_y(20, 2)
+        group_words(23, 1)
+        quantize_y(22, 1)
+        quantize_y(23, 1)

@@ -27,6 +27,7 @@ BLOCKS = GROUPS * HALVES * TILES
 LEAD = 8
 HEAD_PIECES = 7
 HEAD_V = 2
+CONST_AFTER = 3
 EAGER = 2
 AHEAD = 2
 SKIP = ()
@@ -55,15 +56,12 @@ def tile_twin_critic_bellman_targets_b7_kernel(
         w1_s = keep.tile([P, PASSES * 12], F32, name="w1_s")
         ident = keep.tile([P, P], F32, name="ident")
 
-        for t in (f_sc, w2_sc0, w2_sc1):
+        for t in (w2_sc0, f_sc, w2_sc1):
             nc.vector.memset(t[:].rearrange("p c n -> p (c n)").bitcast(I32), 0)
-        nc.vector.memset(rows32[:], 0.0)
 
-        nc.gpsimd.dma_start(out=rows16[12:24, :], in_=b2.rearrange("o (a p) -> (o a) p", p=P))
-        nc.gpsimd.dma_start(out=rows16[0:12, :], in_=b1.rearrange("o (a p) -> (o a) p", p=P))
-        nc.gpsimd.dma_start(out=rows16[24:32, :], in_=disc.rearrange("(a p) o -> a (p o)", p=P))
 
         make_identity(nc, ident[:])
+        nc.scalar.activation(out=rows32[:], in_=ident[:], func=ACT.Identity)
 
         f_codes, w2_codes, w1_raw, rew = {}, {}, {}, {}
 
@@ -79,10 +77,10 @@ def tile_twin_critic_bellman_targets_b7_kernel(
             nc.sync.dma_start(out=t[:].bitcast(I32), in_=src.bitcast(I32))
             w2_codes[g] = t
 
-        def load_scales(t, dram, lo, hi):
-            for q in range(4):
+        def load_scales(t, dram, lo, hi, quadrants, queue):
+            for q in quadrants:
                 src = dram[:, 4 * q : 4 * q + 4, lo:hi].rearrange("c r n -> r c n")
-                nc.sync.dma_start(out=t[32 * q : 32 * q + 4, :, :].bitcast(I32), in_=src.bitcast(I32))
+                queue.dma_start(out=t[32 * q : 32 * q + 4, :, :].bitcast(I32), in_=src.bitcast(I32))
 
         def load_w1(g, c):
             t = keep.tile([P, 4, W], U8, name=f"w1_raw{g}{c}")
@@ -96,19 +94,23 @@ def tile_twin_critic_bellman_targets_b7_kernel(
             nc.sync.dma_start(out=t[:], in_=src)
             rew[g, h] = t
 
-        load_f(0, 0)
+        load_scales(w2_sc0, W2_scales, 0, W, range(1), nc.gpsimd)
+        nc.gpsimd.dma_start(out=rows16[12:24, :], in_=b2.rearrange("o (a p) -> (o a) p", p=P))
+        nc.gpsimd.dma_start(out=rows16[0:12, :], in_=b1.rearrange("o (a p) -> (o a) p", p=P))
+        nc.gpsimd.dma_start(out=rows16[24:32, :], in_=disc.rearrange("(a p) o -> a (p o)", p=P))
+        nc.gpsimd.dma_start(out=s_all[:], in_=W1_scale.rearrange("a b -> (a b)").partition_broadcast(P))
+
         load_w2(0)
-        load_scales(f_sc, F_scales, 0, T)
-        load_scales(w2_sc0, W2_scales, 0, W)
-        load_f(1, 0)
-        load_f(2, 0)
-        nc.sync.dma_start(out=s_all[:], in_=W1_scale.rearrange("a b -> (a b)").partition_broadcast(P))
+        load_scales(w2_sc0, W2_scales, 0, W, range(1, 4), nc.sync)
+        load_scales(f_sc, F_scales, 0, T, range(4), nc.sync)
+        for c in range(PASSES):
+            load_f(c, 0)
         for c in range(PASSES):
             load_w1(0, c)
         for c in range(PASSES):
             load_f(c, 1)
         load_w2(1)
-        load_scales(w2_sc1, W2_scales, W, N)
+        load_scales(w2_sc1, W2_scales, W, N, range(4), nc.sync)
         for c in range(PASSES):
             load_w1(1, c)
         load_reward(0, 0)
@@ -217,7 +219,7 @@ def tile_twin_critic_bellman_targets_b7_kernel(
             if 0 < n <= len(pieces):
                 quantize_piece(n - 1)
 
-        mt_bank, word_bank, y, yb, grouped, y_sc = {}, {}, {}, {}, {}, {}
+        mt_bank, word_bank, y, yb, grouped, y_sc, y_codes = {}, {}, {}, {}, {}, {}, {}
 
         def turn_min(x, b):
             u, i = divmod(x, TILES)
@@ -270,32 +272,39 @@ def tile_twin_critic_bellman_targets_b7_kernel(
             g, h = divmod(u, HALVES)
             if h == 0 and i == 0:
                 y_sc[g] = work.tile([P, T], U8, name="y_sc", bufs=2, align_bytes=64)
-            t = work.tile([P, n * P], U32, name="y_codes", bufs=6, align_bytes=64)
+            if x % 2 == 0:
+                y_codes[x // 2] = work.tile([P, 2 * P], U32, name="y_codes", bufs=6, align_bytes=64)
+            t = y_codes[x // 2]
             lo = W * h + P * i
-            nc.vector.quantize_mx(out=t[:].bitcast(FP8X4), scales=y_sc[g][:, lo : lo + n * P], in_=grouped[x][:])
-            dst = out_1[g].rearrange("p n t -> p (n t)")[:, 4 * lo : 4 * (lo + n * P)]
-            nc.sync.dma_start(out=dst.bitcast(I32), in_=t[:].bitcast(I32))
+            codes = t[:, P * (x % 2) : P * (x % 2 + n)]
+            nc.vector.quantize_mx(out=codes.bitcast(FP8X4), scales=y_sc[g][:, lo : lo + n * P], in_=grouped[x][:])
+            if (x + n) % 2 == 0:
+                end = lo + n * P
+                dst = out_1[g].rearrange("p n t -> p (n t)")[:, 4 * (end - 2 * P) : 4 * end]
+                nc.sync.dma_start(out=dst.bitcast(I32), in_=t[:].bitcast(I32))
             if lo + n * P == T:
                 for q in range(4):
-                    nc.sync.dma_start(
+                    queue = nc.scalar if g == GROUPS - 1 and q % 2 == 1 else nc.sync
+                    queue.dma_start(
                         out=out_2[g, 4 * q : 4 * q + 4, :].bitcast(I32), in_=y_sc[g][32 * q : 32 * q + 4, :].bitcast(I32)
                     )
 
-        nc.scalar.activation(out=rows32[0:32, :], in_=rows16[:], func=ACT.Identity)
-        mm_q2(0, 0)
-        cb = bank(7)
-        nc.tensor.transpose(cb[:, 0:P], rows32[:], ident[:])
+        nc.scalar.copy(out=rows32[0:32, :], in_=rows16[:])
+        for c in range(PASSES):
+            widen(0, c, 0, on_vector=True)
+            widen(0, c, 1, on_vector=(c == HEAD_V))
         for q in range(4):
             nc.vector.tensor_copy(
                 out=w1_s[32 * q : 32 * q + 32, :].rearrange("p (c j) -> p c j", c=PASSES),
                 in_=s_all[32 * q : 32 * q + 32, :].rearrange("p (c q j) -> p c q j", c=PASSES, q=4)[:, :, q, :],
             )
-        nc.vector.tensor_copy(out=cols[:], in_=cb[:, 0:32])
-        for k in range(1, LEAD):
+        for k in range(CONST_AFTER):
             mm_q2(k, k)
-        for c in range(PASSES):
-            widen(0, c, 0, on_vector=True)
-            widen(0, c, 1, on_vector=(c == HEAD_V))
+        cb = bank(7)
+        nc.tensor.transpose(cb[:, 0:P], rows32[:], ident[:])
+        nc.scalar.copy(out=cols[:], in_=cb[:, 0:32])
+        for k in range(CONST_AFTER, LEAD):
+            mm_q2(k, k)
         for k in range(LEAD):
             bias_q2(k)
         for n in range(HEAD_PIECES):
@@ -356,23 +365,23 @@ def tile_twin_critic_bellman_targets_b7_kernel(
         turn_min(16, 4)
         turn_min(17, 5)
         turn_words(14, 2, 6)
+        last_mm(1)
         turn_min(18, 2)
         turn_min(19, 3)
-        last_mm(1)
         last_min(0)
         make_y(16)
         make_y(17)
         group_words(14, 2)
         round_y(16)
         round_y(17)
-        make_y(18)
-        last_min(1)
-        last_mm(2)
         turn_min(20, 4)
-        turn_words(16, 2, 7)
-        turn_min(21, 5)
-        last_mm(3)
+        last_mm(2)
+        last_min(1)
+        make_y(18)
         make_y(19)
+        turn_min(21, 5)
+        turn_words(16, 2, 7)
+        last_mm(3)
         round_y(18)
         round_y(19)
         group_words(16, 2)
@@ -380,6 +389,7 @@ def tile_twin_critic_bellman_targets_b7_kernel(
         quantize_y(14, 2)
         make_y(20)
         round_y(20)
+        quantize_y(16, 2)
         last_min(3)
         turn_min(22, 2)
         turn_words(18, 2, 6)
@@ -392,11 +402,10 @@ def tile_twin_critic_bellman_targets_b7_kernel(
         round_y(22)
         make_y(23)
         group_words(20, 2)
-        quantize_y(16, 2)
+        quantize_y(18, 2)
         round_y(23, on_vector=True)
         turn_words(22, 1, 0)
         turn_words(23, 1, 1)
-        quantize_y(18, 2)
         group_words(22, 1)
         quantize_y(20, 2)
         group_words(23, 1)

@@ -29,6 +29,7 @@ HEAD_PIECES = 7
 HEAD_V = 2
 CONST_AFTER = 3
 EAGER = 2
+WARM = 9
 AHEAD = 2
 SKIP = ()
 
@@ -288,6 +289,10 @@ def tile_twin_critic_bellman_targets_b7_kernel(
                     queue.dma_start(
                         out=out_2[g, 4 * q : 4 * q + 4, :].bitcast(I32), in_=y_sc[g][32 * q : 32 * q + 4, :].bitcast(I32)
                     )
+
+        warm = bank(7)
+        for n in range(WARM):
+            nc.tensor.matmul(warm[:, 0:P], lhsT=ident[:], rhs=ident[:], start=True, stop=True)
 
         nc.scalar.copy(out=rows32[0:32, :], in_=rows16[:])
         for c in range(PASSES):

from contextlib import ExitStack

import concourse.mybir as mybir
from concourse.masks import make_identity

T, K, N = 1024, 1536, 1536
FLOPS = 2 * 2 * T * K * N

F32 = mybir.dt.float32
BF16 = mybir.dt.bfloat16
I32 = mybir.dt.int32
U32 = mybir.dt.uint32
U8 = mybir.dt.uint8
FP8 = mybir.dt.float8_e4m3fn
FP8X4 = mybir.dt.float8_e4m3fn_x4
FP4X4 = mybir.dt.float4_e2m1fn_x4
ALU = mybir.AluOpType
ACT = mybir.ActivationFunctionType

P = 128
W = 512
PASSES = K // W
GROUPS = N // W
HALVES = T // W
TILES = W // P
BLOCKS = GROUPS * HALVES * TILES
LEAD = 8
HEAD_PIECES = 7
HEAD_V = 2
CONST_AFTER = 3
EAGER = 2
WARM = 9
AHEAD = 2
SKIP = ()


def tile_twin_critic_bellman_targets_b7_kernel(
    tc, F_words, F_scales, W1_bytes, W1_scale, W2_words, W2_scales, b1, b2, disc, reward, out_0, out_1, out_2
):
    nc = tc.nc
    with ExitStack() as ctx:
        keep = ctx.enter_context(tc.tile_pool(name="keep", bufs=1))
        work = ctx.enter_context(tc.tile_pool(name="work", bufs=2))
        psum = ctx.enter_context(tc.psum_pool(name="psum", bufs=1))
        ctx.enter_context(tc.manual_schedule())

        def bank(b):
            return psum.tile([P, W], F32, name=f"bank{b}")

        f_sc = keep.tile([P, PASSES, T], U8, name="f_sc", align_bytes=64)
        w2_sc0 = keep.tile([P, PASSES, W], U8, name="w2_sc0", align_bytes=64)
        w2_sc1 = keep.tile([P, PASSES, N - W], U8, name="w2_sc1", align_bytes=64)
        rows32 = keep.tile([P, P], F32, name="rows32")
        rows16 = keep.tile([32, P], BF16, name="rows16")
        cols = keep.tile([P, 32], F32, name="cols")
        s_all = keep.tile([P, 144], F32, name="s_all")
        w1_s = keep.tile([P, PASSES * 12], F32, name="w1_s")
        ident = keep.tile([P, P], F32, name="ident")

        for t in (w2_sc0, f_sc, w2_sc1):
            nc.vector.memset(t[:].rearrange("p c n -> p (c n)").bitcast(I32), 0)


        make_identity(nc, ident[:])
        nc.scalar.activation(out=rows32[:], in_=ident[:], func=ACT.Identity)

        f_codes, w2_codes, w1_raw, rew = {}, {}, {}, {}

        def load_f(c, h):
            t = keep.tile([P, W], U32, name=f"f_codes{c}{h}", align_bytes=64)
            src = F_words[c].rearrange("p n t -> p (n t)")[:, 4 * W * h : 4 * W * (h + 1)]
            nc.sync.dma_start(out=t[:].bitcast(I32), in_=src.bitcast(I32))
            f_codes[c, h] = t

        def load_w2(g):
            t = keep.tile([P, PASSES, 2 * W], U8, name=f"w2_codes{g}", align_bytes=64)
            src = W2_words[:, :, 2 * W * g : 2 * W * (g + 1)].rearrange("c p n -> p c n")
            nc.sync.dma_start(out=t[:].bitcast(I32), in_=src.bitcast(I32))
            w2_codes[g] = t

        def load_scales(t, dram, lo, hi, quadrants, queue):
            for q in quadrants:
                src = dram[:, 4 * q : 4 * q + 4, lo:hi].rearrange("c r n -> r c n")
                queue.dma_start(out=t[32 * q : 32 * q + 4, :, :].bitcast(I32), in_=src.bitcast(I32))

        def load_w1(g, c):
            t = keep.tile([P, 4, W], U8, name=f"w1_raw{g}{c}")
            src = W1_bytes[W * c : W * (c + 1), W * g : W * (g + 1)].rearrange("(p t) n -> p t n", t=4)
            nc.sync.dma_start(out=t[:], in_=src)
            w1_raw[g, c] = t

        def load_reward(g, h):
            t = keep.tile([P, TILES, W], BF16, name=f"rew{g}{h}")
            src = reward[W * h : W * (h + 1), W * g : W * (g + 1)].rearrange("(i p) n -> p i n", p=P)
            nc.sync.dma_start(out=t[:], in_=src)
            rew[g, h] = t

        load_scales(w2_sc0, W2_scales, 0, W, range(1), nc.gpsimd)
        nc.gpsimd.dma_start(out=rows16[12:24, :], in_=b2.rearrange("o (a p) -> (o a) p", p=P))
        nc.gpsimd.dma_start(out=rows16[0:12, :], in_=b1.rearrange("o (a p) -> (o a) p", p=P))
        nc.gpsimd.dma_start(out=rows16[24:32, :], in_=disc.rearrange("(a p) o -> a (p o)", p=P))
        nc.gpsimd.dma_start(out=s_all[:], in_=W1_scale.rearrange("a b -> (a b)").partition_broadcast(P))

        load_w2(0)
        load_scales(w2_sc0, W2_scales, 0, W, range(1, 4), nc.sync)
        load_scales(f_sc, F_scales, 0, T, range(4), nc.sync)
        for c in range(PASSES):
            load_f(c, 0)
        for c in range(PASSES):
            load_w1(0, c)
        for c in range(PASSES):
            load_f(c, 1)
        load_w2(1)
        load_scales(w2_sc1, W2_scales, W, N, range(4), nc.sync)
        for c in range(PASSES):
            load_w1(1, c)
        load_reward(0, 0)
        load_w2(2)
        load_reward(0, 1)
        for c in range(PASSES):
            load_w1(2, c)
        for g in range(1, GROUPS):
            for h in range(HALVES):
                load_reward(g, h)

        def place(k):
            return k // (HALVES * TILES), (k // TILES) % HALVES, k % TILES

        w1_codes, w1_sc, wide, inter, q2_bank, a2, m = {}, {}, {}, {}, {}, {}, {}
        for jj in range(GROUPS * TILES):
            w1_codes[jj] = keep.tile([P, PASSES, P], U32, name=f"w1_codes{jj}", align_bytes=64)
            w1_sc[jj] = keep.tile([P, PASSES, P], U8, name=f"w1_sc{jj}", align_bytes=64)

        def mm_q2(k, b):
            g, h, j = place(k)
            acc = bank(b)
            sc, lo = (w2_sc0, P * j) if g == 0 else (w2_sc1, W * (g - 1) + P * j)
            for c in range(PASSES):
                nc.tensor.matmul_mx(
                    out=acc[:],
                    lhsT=w2_codes[g][:, c, 2 * P * j : 2 * P * (j + 1)].bitcast(FP4X4),
                    lhsT_scale=sc[:, c, lo : lo + P],
                    rhs=f_codes[c, h][:].bitcast(FP8X4),
                    rhs_scale=f_sc[:, c, W * h : W * (h + 1)],
                    start=(c == 0),
                    stop=(c == PASSES - 1),
                )
            q2_bank[k] = acc

        def bias_q2(k, on_vector=False):
            g, h, j = place(k)
            t = work.tile([P, W], F32, name="a2", bufs=LEAD + 2)
            col = cols[:, 12 + TILES * g + j : 13 + TILES * g + j]
            if on_vector:
                nc.vector.tensor_scalar(out=t[:], in0=q2_bank[k][:], scalar1=col, scalar2=None, op0=ALU.add)
            else:
                nc.scalar.activation(out=t[:], in_=q2_bank[k][:], func=ACT.Identity, bias=col)
            a2[k] = t

        def mm_q1(k, acc, lo=0, hi=W):
            g, h, j = place(k)
            jj = TILES * g + j
            for c in range(PASSES):
                nc.tensor.matmul_mx(
                    out=acc,
                    lhsT=w1_codes[jj][:, c, :].bitcast(FP8X4),
                    lhsT_scale=w1_sc[jj][:, c, :],
                    rhs=f_codes[c, h][:, lo:hi].bitcast(FP8X4),
                    rhs_scale=f_sc[:, c, W * h + lo : W * h + hi],
                    start=(c == 0),
                    stop=(c == PASSES - 1),
                )
            return acc

        def take_min(k, acc, lo=0, hi=W):
            g, h, j = place(k)
            if hi - lo == W:
                t = work.tile([P, W], F32, name="m", bufs=2 * TILES)
            else:
                t = work.tile([P, hi - lo], F32, name="m_last", bufs=2 * TILES)
            col = cols[:, TILES * g + j : TILES * g + j + 1]
            nc.vector.scalar_tensor_tensor(
                out=t[:], in0=acc, scalar=col, in1=a2[k][:, lo:hi], op0=ALU.add, op1=ALU.min
            )
            for i in range(lo // P, hi // P):
                m[k, i] = t[:, P * i - lo : P * (i + 1) - lo]

        def widen(g, c, half, on_vector=False):
            if half == 0:
                wide[g, c] = work.tile([P, 4 * W], BF16, name="wide", bufs=4)
            lo, hi = 2 * W * half, 2 * W * (half + 1)
            src = w1_raw[g, c][:].rearrange("p t n -> p (t n)")[:, lo:hi].bitcast(FP8)
            if on_vector:
                nc.vector.tensor_copy(out=wide[g, c][:, lo:hi], in_=src)
            else:
                nc.scalar.copy(out=wide[g, c][:, lo:hi], in_=src)

        pieces = [(0, c, j) for j in range(TILES) for c in range(PASSES)]
        pieces = pieces + [(g, c, j) for g in range(1, GROUPS) for c in range(PASSES) for j in range(TILES)]

        def quantize_piece(n):
            g, c, j = pieces[n]
            jj = TILES * g + j
            nc.vector.quantize_mx(out=w1_codes[jj][:, c, :].bitcast(FP8X4), scales=w1_sc[jj][:, c, :], in_=inter[n][:])

        def prep(n):
            if n < len(pieces):
                g, c, j = pieces[n]
                t = work.tile([P, W], BF16, name="inter", bufs=3, align_bytes=64)
                src = wide[g, c][:].rearrange("p (t n) -> p t n", t=4)[:, :, P * j : P * (j + 1)]
                col = w1_s[:, 12 * c + TILES * g + j : 12 * c + TILES * g + j + 1]
                nc.vector.tensor_scalar(
                    out=t[:].rearrange("p (a i t) -> p a t i", i=4, t=4),
                    in0=src.rearrange("p t (a i) -> p a t i", i=4),
                    scalar1=col,
                    scalar2=None,
                    op0=ALU.mult,
                )
                inter[n] = t
            if 0 < n <= len(pieces):
                quantize_piece(n - 1)

        mt_bank, word_bank, y, yb, grouped, y_sc, y_codes = {}, {}, {}, {}, {}, {}, {}

        def turn_min(x, b):
            u, i = divmod(x, TILES)
            acc = bank(b)
            for j in range(TILES):
                nc.tensor.transpose(acc[:, P * j : P * (j + 1)], m[TILES * u + j, i], ident[:])
            mt_bank[x] = acc

        def make_y(x):
            u, i = divmod(x, TILES)
            g, h = divmod(u, HALVES)
            t = work.tile([P, W], F32, name="y", bufs=6)
            col = cols[:, 24 + TILES * h + i : 25 + TILES * h + i]
            nc.vector.scalar_tensor_tensor(
                out=t[:], in0=mt_bank[x][:], scalar=col, in1=rew[g, h][:, i, :], op0=ALU.mult, op1=ALU.add
            )
            row = W * h + P * i
            nc.sync.dma_start(out=out_0[row : row + P, W * g : W * (g + 1)], in_=t[:])
            y[x] = t

        def round_y(x, on_vector=False):
            t = work.tile([P, W], BF16, name="yb", bufs=6)
            dst = t[:].rearrange("r (u p e) -> r u p e", u=2, e=2)
            src = y[x][:].rearrange("r (p u e) -> r u p e", u=2, e=2)
            if on_vector:
                nc.vector.tensor_copy(out=dst, in_=src)
            else:
                nc.scalar.copy(out=dst, in_=src)
            yb[x] = t

        def turn_words(x, n, b):
            acc = bank(b)
            for ii in range(n):
                words = yb[x + ii][:].bitcast(F32)
                for v in range(2):
                    lo = 2 * P * ii + P * v
                    nc.tensor.transpose(acc[:, lo : lo + P], words[:, P * v : P * (v + 1)], ident[:])
            word_bank[x] = acc

        def group_words(x, n):
            t = work.tile([P, n * W], BF16, name="grouped", bufs=5, align_bytes=64)
            nc.scalar.copy(
                out=t[:].bitcast(F32).rearrange("p (i r u) -> p i r u", i=n, u=2),
                in_=word_bank[x][:, 0 : 2 * P * n].rearrange("p (i u r) -> p i r u", i=n, u=2),
            )
            grouped[x] = t

        def quantize_y(x, n):
            u, i = divmod(x, TILES)
            g, h = divmod(u, HALVES)
            if h == 0 and i == 0:
                y_sc[g] = work.tile([P, T], U8, name="y_sc", bufs=2, align_bytes=64)
            if x % 2 == 0:
                y_codes[x // 2] = work.tile([P, 2 * P], U32, name="y_codes", bufs=6, align_bytes=64)
            t = y_codes[x // 2]
            lo = W * h + P * i
            codes = t[:, P * (x % 2) : P * (x % 2 + n)]
            nc.vector.quantize_mx(out=codes.bitcast(FP8X4), scales=y_sc[g][:, lo : lo + n * P], in_=grouped[x][:])
            if (x + n) % 2 == 0:
                end = lo + n * P
                dst = out_1[g].rearrange("p n t -> p (n t)")[:, 4 * (end - 2 * P) : 4 * end]
                nc.sync.dma_start(out=dst.bitcast(I32), in_=t[:].bitcast(I32))
            if lo + n * P == T:
                for q in range(4):
                    queue = nc.scalar if g == GROUPS - 1 and q % 2 == 1 else nc.sync
                    queue.dma_start(
                        out=out_2[g, 4 * q : 4 * q + 4, :].bitcast(I32), in_=y_sc[g][32 * q : 32 * q + 4, :].bitcast(I32)
                    )

        warm = bank(7)
        for n in range(WARM):
            nc.tensor.matmul(warm[:, 0:P], lhsT=ident[:], rhs=ident[:], start=True, stop=True)

        nc.scalar.copy(out=rows32[0:32, :], in_=rows16[:])
        for c in range(PASSES):
            widen(0, c, 0, on_vector=True)
            widen(0, c, 1, on_vector=(c == HEAD_V))
        for q in range(4):
            nc.vector.tensor_copy(
                out=w1_s[32 * q : 32 * q + 32, :].rearrange("p (c j) -> p c j", c=PASSES),
                in_=s_all[32 * q : 32 * q + 32, :].rearrange("p (c q j) -> p c q j", c=PASSES, q=4)[:, :, q, :],
            )
        for k in range(CONST_AFTER):
            mm_q2(k, k)
        cb = bank(7)
        nc.tensor.transpose(cb[:, 0:P], rows32[:], ident[:])
        nc.scalar.copy(out=cols[:], in_=cb[:, 0:32])
        for k in range(CONST_AFTER, LEAD):
            mm_q2(k, k)
        for k in range(LEAD):
            bias_q2(k)
        for n in range(HEAD_PIECES):
            prep(n)
        done = HEAD_PIECES
        next_q2 = LEAD
        counts = [3 if k < EAGER else 2 for k in range(BLOCKS)]
        first_use = {}
        n = done
        for k in range(BLOCKS):
            for g, c, j in pieces[n : n + counts[k]]:
                first_use.setdefault((g, c), k)
            n = n + counts[k]

        for k in range(BLOCKS - TILES):
            x = 2 * ((k - TILES) // 2)
            if next_q2 < BLOCKS and k not in SKIP:
                mm_q2(next_q2, next_q2 % 2)
                bias_q2(next_q2)
                next_q2 = next_q2 + 1
            if k % 2 == 1 and x >= 0:
                round_y(x + 1)
            for g in range(1, GROUPS):
                for c in range(PASSES):
                    for half in range(2):
                        if k == max(0, first_use[g, c] - AHEAD + half):
                            widen(g, c, half)
            count = counts[k]
            for n in range(done, done + count):
                prep(n)
            if k % 2 == 1 and x >= 2:
                quantize_y(x - 2, 2)
            done = done + count
            take_min(k, mm_q1(k, bank(2 + k % 2)[:]))
            if k % 2 == 0 and x >= 0:
                turn_min(x, 4)
                turn_min(x + 1, 5)
                if x >= 2:
                    turn_words(x - 2, 2, 6 + (x // 2) % 2)
                make_y(x)
                make_y(x + 1)
                if x >= 2:
                    group_words(x - 2, 2)
                round_y(x)

        last_bank = {}

        def last_mm(i):
            last_bank[i] = bank(i % 2)
            for j in range(TILES):
                mm_q1(BLOCKS - TILES + j, last_bank[i][:, P * j : P * (j + 1)], P * i, P * (i + 1))

        def last_min(i):
            for j in range(TILES):
                take_min(BLOCKS - TILES + j, last_bank[i][:, P * j : P * (j + 1)], P * i, P * (i + 1))

        last_mm(0)
        turn_min(16, 4)
        turn_min(17, 5)
        turn_words(14, 2, 6)
        last_mm(1)
        turn_min(18, 2)
        turn_min(19, 3)
        last_min(0)
        make_y(16)
        make_y(17)
        group_words(14, 2)
        round_y(16)
        round_y(17)
        turn_min(20, 4)
        last_mm(2)
        last_min(1)
        make_y(18)
        make_y(19)
        turn_min(21, 5)
        turn_words(16, 2, 7)
        last_mm(3)
        round_y(18)
        round_y(19)
        group_words(16, 2)
        last_min(2)
        quantize_y(14, 2)
        make_y(20)
        round_y(20)
        quantize_y(16, 2)
        last_min(3)
        turn_min(22, 2)
        turn_words(18, 2, 6)
        turn_min(23, 3)
        make_y(21)
        group_words(18, 2)
        round_y(21)
        make_y(22)
        turn_words(20, 2, 7)
        round_y(22)
        make_y(23)
        group_words(20, 2)
        quantize_y(18, 2)
        round_y(23, on_vector=True)
        turn_words(22, 1, 0)
        turn_words(23, 1, 1)
        group_words(22, 1)
        quantize_y(20, 2)
        group_words(23, 1)
        quantize_y(22, 1)
        quantize_y(23, 1)
